import numpy as np, ml_dtypes
CORES = [16,17,18,19,32,33,34,35]
N = 8
import mx_ref
BF = ml_dtypes.bfloat16
def cols(t, e):
    v = np.concatenate([t.reshape(128, -1, 4), np.zeros((128, 1, 4), BF)], axis=1)
    return np.ascontiguousarray(v[:, e]).reshape(128, -1)
def decode(q):
    o = []
    for b in range(4):
        e = np.zeros((128, 128, 4), np.float32); e[np.arange(128), np.arange(128), b] = 1
        o.append(mx_ref.matmul(mx_ref.quantize(e.reshape(128, 512).astype(BF)), q))
    return np.stack(o, axis=2).reshape(128, -1)
def f(rng, *shape):
    return mx_ref.flush((rng.standard_normal(shape, dtype=np.float32) * np.exp2(rng.integers(-2, 3, shape[:-1] + (1,)))).astype(BF))
def wide(rng, *shape, cols=0):
    v = rng.standard_normal(shape, dtype=np.float32) * np.exp2(rng.integers(-12, 13, shape)).astype(np.float32)
    if cols: v *= np.repeat(np.exp2(rng.integers(-cols, cols + 1, shape[:-2] + (1, shape[-1] // 4))) * (rng.random(shape[:-2] + (1, shape[-1] // 4)) > 0.0625), 4, axis=-1).astype(np.float32)
    return mx_ref.flush(v.astype(BF))
T, K = 512, 64
def setup_inputs(rng):
    u = np.zeros((N, 128, 512), BF); u[:, :, :4] = f(rng, N, 128, 4)
    return {"gr": f(rng, N, 128, 4 * T), "u": u}
def raised(rng, chosen):
    d = setup_inputs(rng)
    for r in range(N):
        g = d["gr"][r].astype(np.float32).reshape(128, T, 4)
        sign = np.where(d["u"][r][:, :4].astype(np.float32) < 0, -1, 1).reshape(128, 1, 4) * rng.choice([-1, 1], K).reshape(1, K, 1)
        v = g * np.float32(2.0 ** -8)
        v[:, chosen[r]] = np.abs(g[:, chosen[r]]) * sign
        d["gr"][r] = mx_ref.flush(v.reshape(128, 4 * T).astype(BF))
    return d
def setup_inputs_same(rng):
    d = raised(rng, [rng.permutation(T)[:K]] * N)
    k = rng.permutation(np.concatenate([[12, -12, -11], rng.integers(-12, 13, N - 3)]))
    d["gr"] = mx_ref.flush((d["gr"].astype(np.float32) * np.exp2(k).astype(np.float32).reshape(N, 1, 1)).astype(BF))
    return d
def setup_inputs_apart(rng):
    p = rng.permutation(T)
    return raised(rng, [p[(r * K + np.arange(K)) % T] for r in range(N)])
def setup_inputs_ties(rng):
    d = setup_inputs(rng); n = T // 11
    for r in range(N):
        p = rng.permutation(T)[:11 * n]
        e = np.full(T, -1); e[p] = np.repeat(np.arange(n), 11)
        s = rng.choice([-1, 1], (n, 11)); s[:, 0] = 1; s[:, 1] = -1
        sign = np.ones(T, np.float32); sign[p] = s.reshape(-1)
        d["gr"][r] = (cols(d["gr"][r], e).astype(np.float32).reshape(128, T, 4) * sign.reshape(1, T, 1)).reshape(128, 4 * T).astype(BF)
    return d
def setup_inputs_few(rng):
    d = setup_inputs(rng); p = rng.permutation(N)
    d["u"][p[0]] = 0
    sign = rng.choice([-1, 1], (128, 1, 4))
    d["u"][p[1]][:, :4] = (sign * rng.uniform(1, 4, (128, 1, 4)) * 2.0 ** 28).reshape(128, 4).astype(BF)
    d["gr"][p[1]] = (sign * rng.choice([-1, 1], (1, T, 1)) * rng.uniform(1, 4, (128, T, 4)) * 2.0 ** 28).reshape(128, 4 * T).astype(BF)
    for r in p[2:2 + N // 2]:
        k = rng.permutation(T)[:rng.integers(1, K)]
        e = np.full(T, -1); e[k] = k
        d["gr"][r] = cols(d["gr"][r], e)
    return d
def setup_inputs_spread(rng):
    d = setup_inputs(rng); d["gr"] = wide(rng, N, 128, 4 * T, cols=8); return d
def check_inputs(d):
    return ["u"] if (d["u"][:, :, 4:].astype(np.float32) != 0).any() else []
def reference(gr, u):
    acc = np.zeros((128, T, 4), np.float32); nb = np.zeros((N, K), np.float32); sc = np.zeros((N, 1, K), np.float32)
    er = gr.astype(np.float32).reshape(N, 128, T, 4)
    for s in range(N):
        score = np.abs(mx_ref.matmul(mx_ref.quantize(u[s]), mx_ref.quantize(gr[s]))[0]) + np.float32(0.0)
        e = np.argsort(-score, kind="stable")[:K]
        v = decode(mx_ref.quantize(cols(gr[s], e))).reshape(128, K, 4)
        acc[:, e] = acc[:, e] + v
        er[s][:, e] = er[s][:, e] - v
        nb[s] = e
        sc[s, 0] = score[e]
    return {"acc": np.stack([acc.reshape(128, 4 * T)] * N), "er": er.reshape(N, 128, 4 * T), "nb": np.stack([nb] * N), "sc": sc}

@@ -1,0 +1,305 @@
+from concourse.bass import DstId, RemoteDMATransfer
+from concourse.mybir import dt, AluOpType, AxisListType, ActivationFunctionType
+
+A = AluOpType
+F = ActivationFunctionType
+AX = AxisListType.X
+
+SCRATCH = {
+    "grt": ("sbuf", [128, 2048], "bfloat16"),
+    "uc": ("sbuf", [128, 16], "bfloat16"),
+    "ut": ("sbuf", [128, 512], "bfloat16"),
+    "uq": ("sbuf", [128, 128], "float8_e4m3fn_x4"),
+    "us": ("sbuf", [128, 128], "uint8"),
+    "gq": ("sbuf", [128, 512], "float8_e4m3fn_x4"),
+    "gs": ("sbuf", [128, 512], "uint8"),
+    "ones": ("sbuf", [128, 128], "bfloat16"),
+    "ident": ("sbuf", [128, 128], "bfloat16"),
+    "et": ("sbuf", [128, 2048], "bfloat16"),
+    "eq": ("sbuf", [128, 512], "float8_e4m3fn_x4"),
+    "es": ("sbuf", [128, 512], "uint8"),
+    "pi": ("sbuf", [128, 32], "int32"),
+    "p3": ("sbuf", [128, 32], "int32"),
+    "ic": ("sbuf", [128, 4], "int32"),
+    "fc": ("sbuf", [128, 4], "float32"),
+    "uoff": ("sbuf", [128, 32], "uint16"),
+    "mk": ("sbuf", [128, 4], "float32"),
+    "j0": ("sbuf", [128, 64], "float32"),
+    "jt": ("sbuf", [128, 64], "float32"),
+    "m0": ("sbuf", [128, 64], "float32"),
+    "md": ("sbuf", [128, 64], "float32"),
+    "sl0": ("sbuf", [128, 512], "float32"),
+    "slot": ("sbuf", [128, 512], "float32"),
+    "pt": ("sbuf", [128, 512], "float32"),
+    "pv": ("sbuf", [128, 512], "float32"),
+    "sabs": ("sbuf", [128, 512], "float32"),
+    "scol": ("sbuf", [128, 4], "float32"),
+    "eqt": ("sbuf", [128, 512], "float32"),
+    "eqm": ("sbuf", [128, 512], "float32"),
+    "cmp": ("sbuf", [128, 2048], "float32"),
+    "cnt": ("sbuf", [128, 4], "float32"),
+    "eqc": ("sbuf", [128, 4], "float32"),
+    "ru": ("sbuf", [128, 4], "uint16"),
+    "w": ("sbuf", [128, 512], "float32"),
+    "t1": ("sbuf", [128, 64], "float32"),
+    "xp": ("sbuf", [128, 64], "float32"),
+    "yr": ("sbuf", [128, 64], "float32"),
+    "bb": ("sbuf", [128, 256], "float32"),
+    "bm": ("sbuf", [128, 256], "float32"),
+    "lf": ("sbuf", [128, 32], "float32"),
+    "lx": ("sbuf", [128, 32], "uint16"),
+    "lown": ("sbuf", [128, 4], "uint16"),
+    "ou": ("sbuf", [128, 16], "uint16"),
+    "h": ("sbuf", [128, 512], "bfloat16"),
+    "hq": ("sbuf", [128, 128], "float8_e4m3fn_x4"),
+    "hs": ("sbuf", [128, 128], "uint8"),
+    "ql": ("sbuf", [128, 192], "float8_e4m3fn_x4"),
+    "pl": ("sbuf", [128, 192], "uint8"),
+    "qr": ("sbuf", [128, 256], "float8_e4m3fn_x4"),
+    "pr": ("sbuf", [128, 256], "uint8"),
+    "e32": ("sbuf", [128, 2048], "float32"),
+    "d": ("sbuf", [128, 256], "float32"),
+    "scg": ("sbuf", [128, 64], "float32"),
+    "scp": ("sbuf", [128, 64], "float32"),
+    "x": ("sbuf", [128, 2056], "float32"),
+    "s4": ("sbuf", [128, 512], "float32"),
+    "s2": ("sbuf", [128, 256], "float32"),
+    "s1": ("sbuf", [128, 128], "float32"),
+    "f4": ("sbuf", [128, 512], "float32"),
+    "f2": ("sbuf", [128, 256], "float32"),
+    "f1": ("sbuf", [128, 128], "float32"),
+    "offc": ("sbuf", [128, 128], "uint16"),
+    "offf": ("sbuf", [128, 128], "uint16"),
+    "ac": ("sbuf", [128, 2048], "float32"),
+    "ps": ("psum", [128, 4096], "float32"),
+}
+SEMAPHORES = ["qv", "qs", "qt", "qp", "lu", "l0", "l1", "st", "ll", "lr", "cl", "cr", "loc"]
+
+
+def rank_program(g, core, T, topo):
+    rank = T.rank_of(core)
+    if rank is None:
+        return
+    N = len(T.cores)
+    near = [r for r in range(N) if topo.chip(T.cores[r]) == topo.chip(core)]
+    far = [r for r in range(N) if r not in near]
+    near_others = [r for r in near if r != rank]
+
+    queue = {"v": g.vector, "s": g.scalar, "t": g.tensor, "p": g, "y": g.sync}
+    count = {"v": 0, "s": 0, "t": 0, "p": 0, "st": 0}
+    seen = {}
+
+    def need(e, deps):
+        for sem, val in deps:
+            if seen.get((e, sem), 0) < val:
+                queue[e].wait_ge(T.sem[sem], val)
+                seen[(e, sem)] = val
+
+    def op(e, deps, call):
+        need(e, deps)
+        count[e] += 1
+        call().then_inc(T.sem["q" + e], 1)
+        return ("q" + e, count[e])
+
+    def load(e, out, in_, sem):
+        queue[e].dma_start(out, in_).then_inc(T.sem[sem], 16)
+        return (sem, 16)
+
+    def store(e, deps, out, in_):
+        need(e, deps)
+        queue[e].dma_start(out, in_).then_inc(T.sem["st"], 16)
+        count["st"] += 16
+
+    V, S = g.vector, g.scalar
+
+    def bank(b, n):
+        return T.ps[:, 512 * b:512 * b + n]
+
+    lu = load("y", T.uc[:, 0:16], T.u[:, 0:16], "lu")
+    l1 = load("s", T.grt[:, 1024:2048], T.gr[:, 1024:2048], "l1")
+    l0 = load("y", T.grt[:, 0:1024], T.gr[:, 0:1024], "l0")
+
+    k_pi = op("p", [], lambda: g.iota(T.pi[:, 0:32], [[0, 32]], 0, 1))
+    k_ones = op("v", [], lambda: V.memset(T.ones[:, :], 1.0))
+    k_id = op("p", [k_ones], lambda: g.affine_select(T.ident[:, :], T.ones[:, :], [[-1, 128]], A.is_equal, 0.0, 0, 1))
+    k_j0 = op("p", [], lambda: g.iota(T.j0[:, :], [[128, 4], [1, 16]], 0, 0, allow_small_or_imprecise_dtypes=True))
+    k_m0 = op("p", [], lambda: g.iota(T.m0[:, :], [[1, 16], [0, 4]], 0, 0, allow_small_or_imprecise_dtypes=True))
+    k_sl0 = op("p", [], lambda: g.iota(T.sl0[:, :], [[4, 512]], 8, 0, allow_small_or_imprecise_dtypes=True))
+
+    k_p3 = op("v", [k_pi], lambda: V.tensor_scalar(out=T.p3[:, :], in0=T.pi[:, :], scalar1=3, scalar2=None, op0=A.bitwise_and))
+    for i, bits in ((0, 3), (1, 12), (2, 112), (3, 15)):
+        k_ic = op("v", [k_pi], lambda: V.tensor_scalar(out=T.ic[:, i:i + 1], in0=T.pi[:, 0:1], scalar1=bits, scalar2=None, op0=A.bitwise_and))
+    k_uoff = op("v", [k_p3], lambda: V.tensor_copy(T.uoff[:, :], T.p3[:, :]))
+    k_fc = op("v", [k_ic], lambda: V.tensor_copy(T.fc[:, :], T.ic[:, :]))
+    k_et = op("v", [], lambda: V.memset(T.et[:, :], 0.0))
+    k_e = [op("s", [k_id, k_et], lambda: S.activation(T.et[:, 512 * b + b:512 * (b + 1):4], T.ident[:, :], F.Copy)) for b in range(4)]
+    k_slot = op("s", [k_sl0, k_fc], lambda: S.activation(T.slot[:, :], T.sl0[:, :], F.Identity, bias=T.fc[:, 0:1]))
+    k_pt = op("s", [k_sl0, k_fc], lambda: S.activation(T.pt[:, :], T.sl0[:, :], F.Identity, bias=T.fc[:, 0:1], scale=0.0))
+    k_h0 = op("v", [], lambda: V.memset(T.h[:, 256:512], 0.0))
+    k_x0 = op("v", [], lambda: V.memset(T.x[:, 0:8], 0.0))
+    k_xp = op("v", [], lambda: V.memset(T.xp[:, :], 0.0))
+    k_w = op("v", [], lambda: V.memset(T.w[:, 0:64], 0.0))
+    for jj in range(4):
+        k_mk = op("v", [k_fc], lambda: V.tensor_scalar(out=T.mk[:, jj:jj + 1], in0=T.fc[:, 1:2], scalar1=float(4 * jj), scalar2=None, op0=A.is_equal))
+    k_jt = op("v", [k_j0, k_fc], lambda: V.tensor_scalar(out=T.jt[:, :], in0=T.j0[:, :], scalar1=T.fc[:, 2:3], scalar2=None, op0=A.add))
+    k_md = op("v", [k_m0, k_fc], lambda: V.tensor_scalar(out=T.md[:, :], in0=T.m0[:, :], scalar1=T.fc[:, 3:4], scalar2=None, op0=A.is_equal))
+
+    k_ut = op("v", [lu, k_uoff], lambda: V.tensor_copy(T.ut[:, :], T.uc[:, 0:16].indirect(T.uoff[:, 0:32])))
+    k_uq = op("v", [k_ut], lambda: V.quantize_mx(T.uq[:, 0:128], T.us[:, 0:128], T.ut[:, 0:512]))
+    k_g = [op("v", [ld], lambda: V.quantize_mx(T.gq[:, a:a + 256], T.gs[:, a:a + 256], T.grt[:, 4 * a:4 * a + 1024]))
+           for a, ld in ((0, l0), (256, l1))]
+
+    def column_scores(q):
+        return op("t", [k_uq, k_g[q // 2]], lambda: g.tensor.matmul_mx(
+            bank(1 + q, 128), T.gq[:, 128 * q:128 * q + 128], T.gs[:, 128 * q:128 * q + 128], T.uq[:, 0:128], T.us[:, 0:128], True, True))
+    k_sc = [column_scores(0), column_scores(1)]
+    k_row = op("t", [k_uq] + k_g, lambda: g.tensor.matmul_mx(bank(0, 512), T.uq[:, 0:128], T.us[:, 0:128], T.gq[:, 0:512], T.gs[:, 0:512], True, True))
+    k_sc += [column_scores(2), column_scores(3)]
+
+    k_c0 = op("s", [l0], lambda: S.activation(T.e32[:, 0:512], T.grt[:, 0:512], F.Copy))
+    k_abs = op("s", [k_row], lambda: S.activation(T.sabs[:, :], bank(0, 512), F.Abs))
+    k_scol = [op("v", [k_sc[q]], lambda: V.tensor_reduce(T.scol[:, q:q + 1], bank(1 + q, 1), AX, A.max, apply_absolute_value=True)) for q in range(4)]
+
+    k_eq = [op("v", [k_abs, k_scol[q]], lambda: V.tensor_scalar(
+        out=T.eqt[:, 128 * q:128 * q + 128], in0=T.sabs[:, 128 * q:128 * q + 128], scalar1=T.scol[:, q:q + 1], scalar2=None, op0=A.is_equal)) for q in range(4)]
+    k_eqm = op("p", k_eq, lambda: g.affine_select(T.eqm[:, :], T.eqt[:, :], [[0, 4], [-1, 128]], A.is_gt, 0.0, 0, 1))
+    k_cnt = []
+    for q in range(4):
+        o, m = 512 * q, 128 * q
+        if q:
+            op("v", [k_abs, k_scol[q]], lambda: V.tensor_scalar(out=T.cmp[:, o:o + m], in0=T.sabs[:, 0:m], scalar1=T.scol[:, q:q + 1], scalar2=None, op0=A.is_ge))
+        k = op("v", [k_abs, k_scol[q]], lambda: V.tensor_scalar(out=T.cmp[:, o + m:o + 512], in0=T.sabs[:, m:512], scalar1=T.scol[:, q:q + 1], scalar2=None, op0=A.is_gt))
+        k_cnt.append(op("s", [k], lambda: S.activation(T.cmp[:, o:o + 512], T.cmp[:, o:o + 512], F.Copy, accum_out=T.cnt[:, q:q + 1])))
+    k_eqc = [op("v", [k_eqm], lambda: V.tensor_reduce(T.eqc[:, q:q + 1], T.eqm[:, 128 * q:128 * q + 128], AX, A.add)) for q in range(4)]
+    k_ru = [op("v", [k_cnt[q], k_eqc[q]], lambda: V.tensor_scalar(
+        out=T.ru[:, q:q + 1], in0=T.cnt[:, q:q + 1], scalar1=T.eqc[:, q:q + 1], scalar2=None, op0=A.add)) for q in range(4)]
+
+    k_c1 = op("s", [l0, l1], lambda: S.activation(T.e32[:, 512:2048], T.grt[:, 512:2048], F.Copy))
+
+    k_w1 = op("v", [k_w, k_jt] + k_ru, lambda: V.tensor_copy(T.w[:, 0:512].indirect(T.ru[:, 0:4]), T.jt[:, 0:64]))
+    k_t1 = op("v", [k_w1], lambda: V.transpose(T.t1[:, :], T.w[:, 0:64]))
+    k_x1 = op("v", [k_t1, k_xp], lambda: V.tensor_tensor(T.xp[:, 0:64:32], T.t1[:, 0:64:32], T.t1[:, 16:64:32], A.add))
+    k_y = op("v", [k_x1], lambda: V.transpose(T.yr[:, :], T.xp[:, :]))
+    k_eqz = op("v", k_e, lambda: V.quantize_mx(T.eq[:, 0:512], T.es[:, 0:512], T.et[:, 0:2048]))
+    k_bm = []
+    for a in range(4):
+        k = op("p", [k_y], lambda: g.partition_broadcast(T.bb[:, 64 * a:64 * a + 64], T.yr[32 * a:32 * a + 1, 0:64], 128))
+        k_bm.append(op("v", [k, k_md], lambda: V.tensor_tensor(T.bm[:, 64 * a:64 * a + 64], T.bb[:, 64 * a:64 * a + 64], T.md[:, :], A.mult)))
+    own = 4 * rank
+    k_lf = [op("v", k_bm, lambda: V.tensor_reduce(T.lf[:, own + c:own + c + 1], T.bm[:, c:256:4], AX, A.add)) for c in range(4)]
+
+    far_e = topo.engines(core, T.cores[far[0]])
+    near_e = [e for e in topo.engines(core, T.cores[near_others[0]]) if e not in far_e]
+    far_mask = sum(1 << e for e in far_e)
+    near_mask = sum(1 << e for e in near_e)
+
+    def ids(ranks):
+        return [DstId(rid=topo.addr(T.cores[r])[0], pnc=topo.addr(T.cores[r])[1]) for r in ranks]
+
+    def near_at(r):
+        return [q for q in near if q != r].index(rank)
+
+    def send(deps, src, near_dst, far_dst, near_sem, far_sem):
+        need("p", deps)
+        g.remote_dma_fused([
+            RemoteDMATransfer(dst_ids=ids(far), dma_engine_mask=far_mask, remote_sem=T.sem[far_sem], srcs=[src], dsts=[far_dst(r) for r in far]),
+            RemoteDMATransfer(dst_ids=ids(near_others), dma_engine_mask=near_mask, remote_sem=T.sem[near_sem], srcs=[src], dsts=[near_dst(r) for r in near_others]),
+        ], local_sem=T.sem["loc"])
+
+    send(k_lf, T.lf[:, own:own + 4], lambda r: T.lf[:, own:own + 4], lambda r: T.lf[:, own:own + 4], "ll", "lr")
+    ll = ("ll", len(near_others) * len(near_e))
+    lr = ("lr", len(far) * len(far_e))
+
+    k_ou = [op("v", k_lf, lambda: V.tensor_scalar(out=T.ou[:, 4 * t:4 * t + 4], in0=T.lf[:, own:own + 4], scalar1=4.0, scalar2=float(t), op0=A.mult, op1=A.add)) for t in (2, 0, 3, 1)]
+    k_ou = {2: k_ou[0], 0: k_ou[1], 3: k_ou[2], 1: k_ou[3]}
+    k_h = []
+    for t in (2, 3):
+        k_h.append(op("s", [k_ou[t], l0, l1], lambda: S.activation(T.h[:, t:256:4], T.grt[:, 0:2048].indirect(T.ou[:, 4 * t:4 * t + 4]), F.Copy)))
+    for t in (0, 1):
+        k_h.append(op("v", [k_ou[t], l0, l1], lambda: V.tensor_copy(T.h[:, t:256:4], T.grt[:, 0:2048].indirect(T.ou[:, 4 * t:4 * t + 4]))))
+    k_hq = op("v", k_h + [k_h0], lambda: V.quantize_mx(T.hq[:, 0:128], T.hs[:, 0:128], T.h[:, 0:512]))
+
+    fa = 64 * near.index(rank)
+    send([k_hq], T.hq[:, 0:64].bitcast(dt.uint8),
+         lambda r: T.ql[:, 64 * near_at(r):64 * near_at(r) + 64].bitcast(dt.uint8),
+         lambda r: T.qr[:, fa:fa + 64].bitcast(dt.uint8), "cl", "cr")
+    send([k_hq], T.hs[:, 0:64],
+         lambda r: T.pl[:, 64 * near_at(r):64 * near_at(r) + 64],
+         lambda r: T.pr[:, fa:fa + 64], "cl", "cr")
+    cl = ("cl", 2 * len(near_others) * len(near_e))
+    cr = ("cr", 2 * len(far) * len(far_e))
+
+    def unpack(b, to, q, s, n, deps):
+        return op("t", deps + [k_eqz], lambda: g.tensor.matmul_mx(bank(to, n), T.eq[:, 128 * b:128 * b + 128], T.es[:, 128 * b:128 * b + 128], q[:, 0:n], s[:, 0:n], True, True))
+
+    def xs(r, b, n):
+        return T.x[:, 8 + 256 * r + b:8 + 256 * (r + n):4]
+    k_own = [unpack(b, 4 + b, T.hq, T.hs, 128, [k_hq] + k_scol) for b in range(4)]
+    k_xo = [op("s", [k_own[b]], lambda: S.activation(xs(rank, b, 1), bank(4 + b, 64), F.Copy)) for b in range(4)]
+    k_lown = op("v", k_lf, lambda: V.tensor_copy(T.lown[:, :], T.lf[:, own:own + 4]))
+    k_d = [op("v", [k_xo[b]] + k_h, lambda: V.tensor_tensor(T.d[:, 64 * b:64 * b + 64], T.h[:, b:256:4], xs(rank, b, 1), A.subtract)) for b in range(4)]
+    k_er = op("v", k_d + [k_c0, k_c1] + [k_ou[t] for t in range(4)], lambda: V.tensor_copy(T.e32[:, 0:2048].indirect(T.ou[:, 0:16]), T.d[:, 0:256]))
+    store("y", [k_er], T.er[:, 0:1024], T.e32[:, 0:1024])
+    store("y", [k_er], T.er[:, 1024:2048], T.e32[:, 1024:2048])
+
+    k_scg = op("s", [k_lown, k_abs], lambda: S.activation(T.scg[:, :], T.sabs[:, 0:512].indirect(T.lown[:, 0:4]), F.Copy))
+    k_scp = [op("s", [k_scg], lambda: S.activation(T.scp[0:1, c:64:4], T.scg[0:1, 16 * c:16 * c + 16], F.Copy)) for c in range(4)]
+    store("y", k_scp, T.sc[:, :], T.scp[0:1, 0:64])
+
+    k_lx = {}
+    for part, arrived in ((near, ll), (far, lr)):
+        a = 4 * part[0]
+        k = op("v", [arrived] + (k_lf if part is near else []), lambda: V.tensor_copy(T.lx[:, a:a + 16], T.lf[:, a:a + 16]))
+        for r in part:
+            k_lx[r] = k
+    k_tab = k_pt
+    for s in range(N):
+        lst = T.lx[:, 4 * s:4 * s + 4]
+        if s:
+            k_tab = op("v", [k_tab, k_lx[s]], lambda: V.tensor_copy(T.pv[:, 64 * s:64 * s + 64], T.pt[:, 0:512].indirect(lst)))
+            k_pv = k_tab
+        k_tab = op("v", [k_tab, k_lx[s], k_slot], lambda: V.tensor_copy(T.pt[:, 0:512].indirect(lst), T.slot[:, 64 * s:64 * s + 64]))
+    k4 = [op("s", [k_pv, k_mk], lambda: S.activation(T.s4[:, 112 * j:112 * j + 112], T.pv[:, 64 + j:512:4], F.Copy, scale=T.mk[:, j:j + 1])) for j in range(4)]
+    kf = [op("s", [k_tab, k_mk], lambda: S.activation(T.f4[:, 128 * j:128 * j + 128], T.pt[:, j:512:4], F.Copy, scale=T.mk[:, j:j + 1])) for j in range(4)]
+    k = op("v", k4, lambda: V.tensor_tensor(T.s2[:, 0:224], T.s4[:, 0:224], T.s4[:, 224:448], A.add))
+    k = op("v", [k], lambda: V.tensor_tensor(T.s1[:, 0:112], T.s2[:, 0:112], T.s2[:, 112:224], A.add))
+    k_offc = op("v", [k], lambda: V.tensor_copy(T.offc[:, 0:112], T.s1[:, 0:112]))
+    k = op("v", kf, lambda: V.tensor_tensor(T.f2[:, 0:256], T.f4[:, 0:256], T.f4[:, 256:512], A.add))
+    k = op("v", [k], lambda: V.tensor_tensor(T.f1[:, 0:128], T.f2[:, 0:128], T.f2[:, 128:256], A.add))
+    k_offf = op("v", [k], lambda: V.tensor_copy(T.offf[:, 0:128], T.f1[:, 0:128]))
+    for s in near + far:
+        store("y", k_lf if s == rank else [ll if s in near else lr], T.nb[s:s + 1, 0:64], T.lf[0:16, 4 * s:4 * s + 4])
+
+    k_near = [unpack(b, b, T.ql, T.pl, 192, [cl, k_abs] + k_scol) for b in range(4)]
+    k_far = [unpack(b, 4 + b, T.qr, T.pr, 256, [cr] + k_xo) for b in range(4)]
+    k_v = []
+    for b in range(4):
+        i = near.index(rank)
+        for at, first, n in ((0, near[0], i), (i, rank + 1, len(near) - 1 - i)):
+            if n:
+                k_v.append(op("s", [k_near[b]], lambda: S.activation(xs(first, b, n), T.ps[:, 512 * b + 64 * at:512 * b + 64 * (at + n)], F.Copy)))
+    k_v += k_xo
+    k_ready = {r: k_v for r in near}
+    k_fv = [op("s", [k_far[b]], lambda: S.activation(xs(far[0], b, 4), bank(4 + b, 256), F.Copy)) for b in (2, 3)]
+
+    k_sum = []
+    k = k_x0
+    for s in range(N):
+        if s == far[0]:
+            k_fv += [op("v", [k_far[b]], lambda: V.tensor_copy(xs(far[0], b, 4), bank(4 + b, 256))) for b in (0, 1)]
+            for r in far:
+                k_ready[r] = k_fv
+        if s:
+            a = 8 + 256 * s
+            k = op("v", [k, k_offc, k_x0] + k_ready[s] + k_ready[0] + k_d, lambda: V.tensor_tensor(
+                T.x[:, a:a + 256], T.x[:, 0:a].indirect(T.offc[:, 16 * (s - 1):16 * s]), T.x[:, a:a + 256], A.add))
+    for i in range(4):
+        e = "v" if i % 2 == 0 else "s"
+        out, src = T.ac[:, 512 * i:512 * i + 512], T.x[:, 0:2056].indirect(T.offf[:, 32 * i:32 * i + 32])
+        if e == "v":
+            ka = op("v", [k, k_offf], lambda: V.tensor_copy(out, src))
+        else:
+            ka = op("s", [k, k_offf], lambda: S.activation(out, src, F.Copy))
+        store("y" if i != 3 else "s", [ka], T.acc[:, 512 * i:512 * i + 512], out)
+
+    need("p", [("q" + e, count[e]) for e in "vstp"] + [("st", count["st"]), ("loc", 3 * (len(far_e) + len(near_e)))])

@@ -4,6 +4,8 @@ from concourse.mybir import dt, AluOpType, AxisListType, ActivationFunctionType
 A = AluOpType
 F = ActivationFunctionType
 AX = AxisListType.X
+STEP = 4096.0
+DROP = 1048576.0
 
 SCRATCH = {
     "grt": ("sbuf", [128, 2048], "bfloat16"),
@@ -23,21 +25,26 @@ SCRATCH = {
     "ic": ("sbuf", [128, 4], "int32"),
     "fc": ("sbuf", [128, 4], "float32"),
     "uoff": ("sbuf", [128, 32], "uint16"),
-    "mk": ("sbuf", [128, 4], "float32"),
     "j0": ("sbuf", [128, 64], "float32"),
     "jt": ("sbuf", [128, 64], "float32"),
     "m0": ("sbuf", [128, 64], "float32"),
     "md": ("sbuf", [128, 64], "float32"),
+    "n0": ("sbuf", [128, 512], "float32"),
+    "n1": ("sbuf", [128, 512], "float32"),
+    "stp": ("sbuf", [128, 512], "float32"),
+    "cor": ("sbuf", [128, 1], "float32"),
     "sl0": ("sbuf", [128, 512], "float32"),
     "slot": ("sbuf", [128, 512], "float32"),
     "pt": ("sbuf", [128, 512], "float32"),
     "pv": ("sbuf", [128, 512], "float32"),
+    "pts": ("sbuf", [128, 512], "float32"),
+    "pvs": ("sbuf", [128, 448], "float32"),
     "sabs": ("sbuf", [128, 512], "float32"),
     "scol": ("sbuf", [128, 4], "float32"),
     "eqt": ("sbuf", [128, 512], "float32"),
     "eqm": ("sbuf", [128, 512], "float32"),
     "cmp": ("sbuf", [128, 2048], "float32"),
-    "cnt": ("sbuf", [128, 4], "float32"),
+    "cnt": ("sbuf", [128, 8], "float32"),
     "eqc": ("sbuf", [128, 4], "float32"),
     "ru": ("sbuf", [128, 4], "uint16"),
     "w": ("sbuf", [128, 512], "float32"),
@@ -62,13 +69,7 @@ SCRATCH = {
     "scg": ("sbuf", [128, 64], "float32"),
     "scp": ("sbuf", [128, 64], "float32"),
     "x": ("sbuf", [128, 2056], "float32"),
-    "s4": ("sbuf", [128, 512], "float32"),
-    "s2": ("sbuf", [128, 256], "float32"),
-    "s1": ("sbuf", [128, 128], "float32"),
-    "f4": ("sbuf", [128, 512], "float32"),
-    "f2": ("sbuf", [128, 256], "float32"),
-    "f1": ("sbuf", [128, 128], "float32"),
-    "offc": ("sbuf", [128, 128], "uint16"),
+    "offc": ("sbuf", [128, 112], "uint16"),
     "offf": ("sbuf", [128, 128], "uint16"),
     "ac": ("sbuf", [128, 2048], "float32"),
     "ps": ("psum", [128, 4096], "float32"),
@@ -90,10 +91,13 @@ def rank_program(g, core, T, topo):
     seen = {}
 
     def need(e, deps):
+        top = {}
         for sem, val in deps:
-            if seen.get((e, sem), 0) < val:
-                queue[e].wait_ge(T.sem[sem], val)
-                seen[(e, sem)] = val
+            top[sem] = max(val, top.get(sem, 0))
+        for sem in top:
+            if seen.get((e, sem), 0) < top[sem]:
+                queue[e].wait_ge(T.sem[sem], top[sem])
+                seen[(e, sem)] = top[sem]
 
     def op(e, deps, call):
         need(e, deps)
@@ -115,64 +119,91 @@ def rank_program(g, core, T, topo):
     def bank(b, n):
         return T.ps[:, 512 * b:512 * b + n]
 
-    lu = load("y", T.uc[:, 0:16], T.u[:, 0:16], "lu")
-    l1 = load("s", T.grt[:, 1024:2048], T.gr[:, 1024:2048], "l1")
-    l0 = load("y", T.grt[:, 0:1024], T.gr[:, 0:1024], "l0")
+    def vs(deps, out, in0, s1, op0, s2=None, op1=None):
+        if op1 is None:
+            return op("v", deps, lambda: V.tensor_scalar(out=out, in0=in0, scalar1=s1, scalar2=None, op0=op0))
+        return op("v", deps, lambda: V.tensor_scalar(out=out, in0=in0, scalar1=s1, scalar2=s2, op0=op0, op1=op1))
 
+    lu = load("y", T.uc[:, 0:16], T.u[:, 0:16], "lu")
+    l0 = load("y", T.grt[:, 0:1024], T.gr[:, 0:1024], "l0")
+    l1 = load("y", T.grt[:, 1024:2048], T.gr[:, 1024:2048], "l1")
+
+    def whole(out, pattern, base=0):
+        return op("p", [], lambda: g.iota(out, pattern, base, 0, allow_small_or_imprecise_dtypes=True))
     k_pi = op("p", [], lambda: g.iota(T.pi[:, 0:32], [[0, 32]], 0, 1))
     k_ones = op("v", [], lambda: V.memset(T.ones[:, :], 1.0))
     k_id = op("p", [k_ones], lambda: g.affine_select(T.ident[:, :], T.ones[:, :], [[-1, 128]], A.is_equal, 0.0, 0, 1))
-    k_j0 = op("p", [], lambda: g.iota(T.j0[:, :], [[128, 4], [1, 16]], 0, 0, allow_small_or_imprecise_dtypes=True))
-    k_m0 = op("p", [], lambda: g.iota(T.m0[:, :], [[1, 16], [0, 4]], 0, 0, allow_small_or_imprecise_dtypes=True))
-    k_sl0 = op("p", [], lambda: g.iota(T.sl0[:, :], [[4, 512]], 8, 0, allow_small_or_imprecise_dtypes=True))
+    k_j0 = whole(T.j0[:, :], [[128, 4], [1, 16]])
+    k_m0 = whole(T.m0[:, :], [[1, 16], [0, 4]])
+    k_sl0 = whole(T.sl0[:, :], [[4, 512]], 8)
+    k_n0 = whole(T.n0[:, :], [[0, 128], [4, 4]])
 
-    k_p3 = op("v", [k_pi], lambda: V.tensor_scalar(out=T.p3[:, :], in0=T.pi[:, :], scalar1=3, scalar2=None, op0=A.bitwise_and))
+    k_p3 = vs([k_pi], T.p3[:, :], T.pi[:, :], 3, A.bitwise_and)
     for i, bits in ((0, 3), (1, 12), (2, 112), (3, 15)):
-        k_ic = op("v", [k_pi], lambda: V.tensor_scalar(out=T.ic[:, i:i + 1], in0=T.pi[:, 0:1], scalar1=bits, scalar2=None, op0=A.bitwise_and))
+        k_ic = vs([k_pi], T.ic[:, i:i + 1], T.pi[:, 0:1], bits, A.bitwise_and)
     k_uoff = op("v", [k_p3], lambda: V.tensor_copy(T.uoff[:, :], T.p3[:, :]))
     k_fc = op("v", [k_ic], lambda: V.tensor_copy(T.fc[:, :], T.ic[:, :]))
     k_et = op("v", [], lambda: V.memset(T.et[:, :], 0.0))
     k_e = [op("s", [k_id, k_et], lambda: S.activation(T.et[:, 512 * b + b:512 * (b + 1):4], T.ident[:, :], F.Copy)) for b in range(4)]
     k_slot = op("s", [k_sl0, k_fc], lambda: S.activation(T.slot[:, :], T.sl0[:, :], F.Identity, bias=T.fc[:, 0:1]))
     k_pt = op("s", [k_sl0, k_fc], lambda: S.activation(T.pt[:, :], T.sl0[:, :], F.Identity, bias=T.fc[:, 0:1], scale=0.0))
-    k_h0 = op("v", [], lambda: V.memset(T.h[:, 256:512], 0.0))
-    k_x0 = op("v", [], lambda: V.memset(T.x[:, 0:8], 0.0))
-    k_xp = op("v", [], lambda: V.memset(T.xp[:, :], 0.0))
-    k_w = op("v", [], lambda: V.memset(T.w[:, 0:64], 0.0))
-    for jj in range(4):
-        k_mk = op("v", [k_fc], lambda: V.tensor_scalar(out=T.mk[:, jj:jj + 1], in0=T.fc[:, 1:2], scalar1=float(4 * jj), scalar2=None, op0=A.is_equal))
-    k_jt = op("v", [k_j0, k_fc], lambda: V.tensor_scalar(out=T.jt[:, :], in0=T.j0[:, :], scalar1=T.fc[:, 2:3], scalar2=None, op0=A.add))
-    k_md = op("v", [k_m0, k_fc], lambda: V.tensor_scalar(out=T.md[:, :], in0=T.m0[:, :], scalar1=T.fc[:, 3:4], scalar2=None, op0=A.is_equal))
 
     k_ut = op("v", [lu, k_uoff], lambda: V.tensor_copy(T.ut[:, :], T.uc[:, 0:16].indirect(T.uoff[:, 0:32])))
     k_uq = op("v", [k_ut], lambda: V.quantize_mx(T.uq[:, 0:128], T.us[:, 0:128], T.ut[:, 0:512]))
-    k_g = [op("v", [ld], lambda: V.quantize_mx(T.gq[:, a:a + 256], T.gs[:, a:a + 256], T.grt[:, 4 * a:4 * a + 1024]))
-           for a, ld in ((0, l0), (256, l1))]
 
-    def column_scores(q):
-        return op("t", [k_uq, k_g[q // 2]], lambda: g.tensor.matmul_mx(
-            bank(1 + q, 128), T.gq[:, 128 * q:128 * q + 128], T.gs[:, 128 * q:128 * q + 128], T.uq[:, 0:128], T.us[:, 0:128], True, True))
-    k_sc = [column_scores(0), column_scores(1)]
-    k_row = op("t", [k_uq] + k_g, lambda: g.tensor.matmul_mx(bank(0, 512), T.uq[:, 0:128], T.us[:, 0:128], T.gq[:, 0:512], T.gs[:, 0:512], True, True))
-    k_sc += [column_scores(2), column_scores(3)]
-
+    def pack(a, ld):
+        return op("v", [ld], lambda: V.quantize_mx(T.gq[:, a:a + 256], T.gs[:, a:a + 256], T.grt[:, 4 * a:4 * a + 1024]))
+    k_g = [pack(0, l0)]
+    k_w = op("v", [], lambda: V.memset(T.w[:, 0:64], 0.0))
+    k_xp = op("v", [], lambda: V.memset(T.xp[:, :], 0.0))
+    k_jt = vs([k_j0, k_fc], T.jt[:, :], T.j0[:, :], T.fc[:, 2:3], A.add)
+    k_md = vs([k_m0, k_fc], T.md[:, :], T.m0[:, :], T.fc[:, 3:4], A.is_equal)
+    k_g.append(pack(256, l1))
     k_c0 = op("s", [l0], lambda: S.activation(T.e32[:, 0:512], T.grt[:, 0:512], F.Copy))
-    k_abs = op("s", [k_row], lambda: S.activation(T.sabs[:, :], bank(0, 512), F.Abs))
-    k_scol = [op("v", [k_sc[q]], lambda: V.tensor_reduce(T.scol[:, q:q + 1], bank(1 + q, 1), AX, A.max, apply_absolute_value=True)) for q in range(4)]
+    k_abs, k_sc = [], []
+    for i, b in ((0, 0), (1, 5)):
+        a = 256 * i
+        k = op("t", [k_uq, k_g[i]], lambda: g.tensor.matmul_mx(bank(b, 256), T.uq[:, 0:128], T.us[:, 0:128], T.gq[:, a:a + 256], T.gs[:, a:a + 256], True, True))
+        k_abs.append(op("s", [k], lambda: S.activation(T.sabs[:, a:a + 256], bank(b, 256), F.Abs)))
+        for q in (2 * i, 2 * i + 1):
+            k_sc.append(op("t", [k_uq, k_g[i]], lambda: g.tensor.matmul_mx(
+                bank(1 + q, 128), T.gq[:, 128 * q:128 * q + 128], T.gs[:, 128 * q:128 * q + 128], T.uq[:, 0:128], T.us[:, 0:128], True, True)))
 
-    k_eq = [op("v", [k_abs, k_scol[q]], lambda: V.tensor_scalar(
-        out=T.eqt[:, 128 * q:128 * q + 128], in0=T.sabs[:, 128 * q:128 * q + 128], scalar1=T.scol[:, q:q + 1], scalar2=None, op0=A.is_equal)) for q in range(4)]
+    k_scol, k_eq, k_cnt = [], [], {}
+
+    def column_score(q):
+        k_scol.append(op("v", [k_sc[q]], lambda: V.tensor_reduce(T.scol[:, q:q + 1], bank(1 + q, 1), AX, A.max, apply_absolute_value=True)))
+
+    def equal_scores(q):
+        k_eq.append(vs([k_abs[q // 2], k_scol[q]], T.eqt[:, 128 * q:128 * q + 128], T.sabs[:, 128 * q:128 * q + 128], T.scol[:, q:q + 1], A.is_equal))
+
+    def larger_scores(q, i):
+        lo, hi = 256 * i, 256 * i + 256
+        cut = min(max(128 * q, lo), hi)
+        for a, b, how in ((lo, cut, A.is_ge), (cut, hi, A.is_gt)):
+            if a < b:
+                k = vs([k_abs[i], k_scol[q]], T.cmp[:, 512 * q + a:512 * q + b], T.sabs[:, a:b], T.scol[:, q:q + 1], how)
+        part = T.cmp[:, 512 * q + lo:512 * q + hi]
+        k_cnt[(q, i)] = op("s", [k], lambda: S.activation(part, part, F.Copy, accum_out=T.cnt[:, 4 * i + q:4 * i + q + 1]))
+    for q in (0, 1):
+        column_score(q)
+    for q in (0, 1):
+        equal_scores(q)
+    for q in (0, 1):
+        larger_scores(q, 0)
+    for q in (2, 3):
+        column_score(q)
+    for q in (2, 3):
+        equal_scores(q)
     k_eqm = op("p", k_eq, lambda: g.affine_select(T.eqm[:, :], T.eqt[:, :], [[0, 4], [-1, 128]], A.is_gt, 0.0, 0, 1))
-    k_cnt = []
-    for q in range(4):
-        o, m = 512 * q, 128 * q
-        if q:
-            op("v", [k_abs, k_scol[q]], lambda: V.tensor_scalar(out=T.cmp[:, o:o + m], in0=T.sabs[:, 0:m], scalar1=T.scol[:, q:q + 1], scalar2=None, op0=A.is_ge))
-        k = op("v", [k_abs, k_scol[q]], lambda: V.tensor_scalar(out=T.cmp[:, o + m:o + 512], in0=T.sabs[:, m:512], scalar1=T.scol[:, q:q + 1], scalar2=None, op0=A.is_gt))
-        k_cnt.append(op("s", [k], lambda: S.activation(T.cmp[:, o:o + 512], T.cmp[:, o:o + 512], F.Copy, accum_out=T.cnt[:, q:q + 1])))
-    k_eqc = [op("v", [k_eqm], lambda: V.tensor_reduce(T.eqc[:, q:q + 1], T.eqm[:, 128 * q:128 * q + 128], AX, A.add)) for q in range(4)]
-    k_ru = [op("v", [k_cnt[q], k_eqc[q]], lambda: V.tensor_scalar(
-        out=T.ru[:, q:q + 1], in0=T.cnt[:, q:q + 1], scalar1=T.eqc[:, q:q + 1], scalar2=None, op0=A.add)) for q in range(4)]
+    for q, i in ((0, 1), (1, 1), (2, 0), (2, 1), (3, 0), (3, 1)):
+        larger_scores(q, i)
+
+    def eq_part(q):
+        return T.eqm[:, 128 * q:128 * q + 128]
+    k_eqc = [op("v", [k_eqm], lambda: V.tensor_reduce(T.eqc[:, q:q + 1], eq_part(q), AX, A.add)) for q in range(3)]
+    k_eqc.append(op("s", [k_eqm], lambda: S.activation(eq_part(3), eq_part(3), F.Copy, accum_out=T.eqc[:, 3:4])))
+    k_ru = [vs([k_cnt[(q, 0)], k_cnt[(q, 1)], k_eqc[q]], T.ru[:, q:q + 1], T.cnt[:, q:q + 1], T.cnt[:, 4 + q:5 + q], A.add, T.eqc[:, q:q + 1], A.add) for q in range(4)]
 
     k_c1 = op("s", [l0, l1], lambda: S.activation(T.e32[:, 512:2048], T.grt[:, 512:2048], F.Copy))
 
@@ -180,11 +211,15 @@ def rank_program(g, core, T, topo):
     k_t1 = op("v", [k_w1], lambda: V.transpose(T.t1[:, :], T.w[:, 0:64]))
     k_x1 = op("v", [k_t1, k_xp], lambda: V.tensor_tensor(T.xp[:, 0:64:32], T.t1[:, 0:64:32], T.t1[:, 16:64:32], A.add))
     k_y = op("v", [k_x1], lambda: V.transpose(T.yr[:, :], T.xp[:, :]))
-    k_eqz = op("v", k_e, lambda: V.quantize_mx(T.eq[:, 0:512], T.es[:, 0:512], T.et[:, 0:2048]))
+    k_h0 = op("v", [], lambda: V.memset(T.h[:, 256:512], 0.0))
+    k_x0 = op("v", [], lambda: V.memset(T.x[:, 0:8], 0.0))
+    k_cor = vs([k_fc], T.cor[:, :], T.fc[:, 1:2], STEP / 4, A.mult, -3 * STEP, A.add)
     k_bm = []
     for a in range(4):
         k = op("p", [k_y], lambda: g.partition_broadcast(T.bb[:, 64 * a:64 * a + 64], T.yr[32 * a:32 * a + 1, 0:64], 128))
         k_bm.append(op("v", [k, k_md], lambda: V.tensor_tensor(T.bm[:, 64 * a:64 * a + 64], T.bb[:, 64 * a:64 * a + 64], T.md[:, :], A.mult)))
+        if a == 0:
+            k_eqz = op("v", k_e, lambda: V.quantize_mx(T.eq[:, 0:512], T.es[:, 0:512], T.et[:, 0:2048]))
     own = 4 * rank
     k_lf = [op("v", k_bm, lambda: V.tensor_reduce(T.lf[:, own + c:own + c + 1], T.bm[:, c:256:4], AX, A.add)) for c in range(4)]
 
@@ -192,6 +227,7 @@ def rank_program(g, core, T, topo):
     near_e = [e for e in topo.engines(core, T.cores[near_others[0]]) if e not in far_e]
     far_mask = sum(1 << e for e in far_e)
     near_mask = sum(1 << e for e in near_e)
+    left = ("loc", 3 * (len(far_e) + len(near_e)))
 
     def ids(ranks):
         return [DstId(rid=topo.addr(T.cores[r])[0], pnc=topo.addr(T.cores[r])[1]) for r in ranks]
@@ -210,8 +246,7 @@ def rank_program(g, core, T, topo):
     ll = ("ll", len(near_others) * len(near_e))
     lr = ("lr", len(far) * len(far_e))
 
-    k_ou = [op("v", k_lf, lambda: V.tensor_scalar(out=T.ou[:, 4 * t:4 * t + 4], in0=T.lf[:, own:own + 4], scalar1=4.0, scalar2=float(t), op0=A.mult, op1=A.add)) for t in (2, 0, 3, 1)]
-    k_ou = {2: k_ou[0], 0: k_ou[1], 3: k_ou[2], 1: k_ou[3]}
+    k_ou = {t: vs(k_lf, T.ou[:, 4 * t:4 * t + 4], T.lf[:, own:own + 4], 4.0, A.mult, float(t), A.add) for t in (2, 0, 3, 1)}
     k_h = []
     for t in (2, 3):
         k_h.append(op("s", [k_ou[t], l0, l1], lambda: S.activation(T.h[:, t:256:4], T.grt[:, 0:2048].indirect(T.ou[:, 4 * t:4 * t + 4]), F.Copy)))
@@ -229,22 +264,22 @@ def rank_program(g, core, T, topo):
     cl = ("cl", 2 * len(near_others) * len(near_e))
     cr = ("cr", 2 * len(far) * len(far_e))
 
-    def unpack(b, to, q, s, n, deps):
-        return op("t", deps + [k_eqz], lambda: g.tensor.matmul_mx(bank(to, n), T.eq[:, 128 * b:128 * b + 128], T.es[:, 128 * b:128 * b + 128], q[:, 0:n], s[:, 0:n], True, True))
+    def unpack(b, to, q, s, a, n, deps):
+        return op("t", deps + [k_eqz], lambda: g.tensor.matmul_mx(bank(to, n), T.eq[:, 128 * b:128 * b + 128], T.es[:, 128 * b:128 * b + 128], q[:, a:a + n], s[:, a:a + n], True, True))
 
     def xs(r, b, n):
         return T.x[:, 8 + 256 * r + b:8 + 256 * (r + n):4]
-    k_own = [unpack(b, 4 + b, T.hq, T.hs, 128, [k_hq] + k_scol) for b in range(4)]
+    k_own = [unpack(b, 4 + b, T.hq, T.hs, 0, 128, [k_hq] + k_scol + k_abs) for b in range(4)]
     k_xo = [op("s", [k_own[b]], lambda: S.activation(xs(rank, b, 1), bank(4 + b, 64), F.Copy)) for b in range(4)]
     k_lown = op("v", k_lf, lambda: V.tensor_copy(T.lown[:, :], T.lf[:, own:own + 4]))
+    k_n1 = vs([k_n0, k_fc], T.n1[:, :], T.n0[:, :], T.fc[:, 1:2], A.is_equal, -(DROP + STEP), A.mult)
     k_d = [op("v", [k_xo[b]] + k_h, lambda: V.tensor_tensor(T.d[:, 64 * b:64 * b + 64], T.h[:, b:256:4], xs(rank, b, 1), A.subtract)) for b in range(4)]
     k_er = op("v", k_d + [k_c0, k_c1] + [k_ou[t] for t in range(4)], lambda: V.tensor_copy(T.e32[:, 0:2048].indirect(T.ou[:, 0:16]), T.d[:, 0:256]))
-    store("y", [k_er], T.er[:, 0:1024], T.e32[:, 0:1024])
-    store("y", [k_er], T.er[:, 1024:2048], T.e32[:, 1024:2048])
 
-    k_scg = op("s", [k_lown, k_abs], lambda: S.activation(T.scg[:, :], T.sabs[:, 0:512].indirect(T.lown[:, 0:4]), F.Copy))
+    k_scg = op("s", [k_lown] + k_abs, lambda: S.activation(T.scg[:, :], T.sabs[:, 0:512].indirect(T.lown[:, 0:4]), F.Copy))
     k_scp = [op("s", [k_scg], lambda: S.activation(T.scp[0:1, c:64:4], T.scg[0:1, 16 * c:16 * c + 16], F.Copy)) for c in range(4)]
     store("y", k_scp, T.sc[:, :], T.scp[0:1, 0:64])
+    k_stp = op("s", [k_n1], lambda: S.activation(T.stp[:, :], T.n1[:, :], F.Identity, bias=STEP))
 
     k_lx = {}
     for part, arrived in ((near, ll), (far, lr)):
@@ -259,47 +294,48 @@ def rank_program(g, core, T, topo):
             k_tab = op("v", [k_tab, k_lx[s]], lambda: V.tensor_copy(T.pv[:, 64 * s:64 * s + 64], T.pt[:, 0:512].indirect(lst)))
             k_pv = k_tab
         k_tab = op("v", [k_tab, k_lx[s], k_slot], lambda: V.tensor_copy(T.pt[:, 0:512].indirect(lst), T.slot[:, 64 * s:64 * s + 64]))
-    k4 = [op("s", [k_pv, k_mk], lambda: S.activation(T.s4[:, 112 * j:112 * j + 112], T.pv[:, 64 + j:512:4], F.Copy, scale=T.mk[:, j:j + 1])) for j in range(4)]
-    kf = [op("s", [k_tab, k_mk], lambda: S.activation(T.f4[:, 128 * j:128 * j + 128], T.pt[:, j:512:4], F.Copy, scale=T.mk[:, j:j + 1])) for j in range(4)]
-    k = op("v", k4, lambda: V.tensor_tensor(T.s2[:, 0:224], T.s4[:, 0:224], T.s4[:, 224:448], A.add))
-    k = op("v", [k], lambda: V.tensor_tensor(T.s1[:, 0:112], T.s2[:, 0:112], T.s2[:, 112:224], A.add))
-    k_offc = op("v", [k], lambda: V.tensor_copy(T.offc[:, 0:112], T.s1[:, 0:112]))
-    k = op("v", kf, lambda: V.tensor_tensor(T.f2[:, 0:256], T.f4[:, 0:256], T.f4[:, 256:512], A.add))
-    k = op("v", [k], lambda: V.tensor_tensor(T.f1[:, 0:128], T.f2[:, 0:128], T.f2[:, 128:256], A.add))
-    k_offf = op("v", [k], lambda: V.tensor_copy(T.offf[:, 0:128], T.f1[:, 0:128]))
+    k_pvs = op("v", [k_pv, k_stp], lambda: V.tensor_tensor_scan(T.pvs[:, 0:448], T.stp[:, 0:448], T.pv[:, 64:512], 0.0, A.add, A.max))
+    k_offc = vs([k_pvs, k_cor], T.offc[:, 0:112], T.pvs[:, 3:448:4], T.cor[:, 0:1], A.add)
+
+    def final_offsets():
+        k = op("v", [k_tab, k_stp], lambda: V.tensor_tensor_scan(T.pts[:, 0:512], T.stp[:, 0:512], T.pt[:, 0:512], 0.0, A.add, A.max))
+        return vs([k, k_cor], T.offf[:, 0:128], T.pts[:, 3:512:4], T.cor[:, 0:1], A.add)
     for s in near + far:
         store("y", k_lf if s == rank else [ll if s in near else lr], T.nb[s:s + 1, 0:64], T.lf[0:16, 4 * s:4 * s + 4])
+    store("y", [k_er, left], T.er[:, 0:1024], T.e32[:, 0:1024])
+    store("y", [k_er, left], T.er[:, 1024:2048], T.e32[:, 1024:2048])
 
-    k_near = [unpack(b, b, T.ql, T.pl, 192, [cl, k_abs] + k_scol) for b in range(4)]
-    k_far = [unpack(b, 4 + b, T.qr, T.pr, 256, [cr] + k_xo) for b in range(4)]
+    k_near = [unpack(b, b, T.ql, T.pl, 0, 192, [cl] + k_abs + k_scol) for b in range(4)]
     k_v = []
     for b in range(4):
         i = near.index(rank)
         for at, first, n in ((0, near[0], i), (i, rank + 1, len(near) - 1 - i)):
             if n:
                 k_v.append(op("s", [k_near[b]], lambda: S.activation(xs(first, b, n), T.ps[:, 512 * b + 64 * at:512 * b + 64 * (at + n)], F.Copy)))
+    k_far1 = [unpack(b, 4 + b, T.qr, T.pr, 0, 128, [cr] + k_xo) for b in range(4)]
+    k_far2 = [unpack(b, b, T.qr, T.pr, 128, 128, [cr] + k_v) for b in range(4)]
     k_v += k_xo
     k_ready = {r: k_v for r in near}
-    k_fv = [op("s", [k_far[b]], lambda: S.activation(xs(far[0], b, 4), bank(4 + b, 256), F.Copy)) for b in (2, 3)]
+    k_fv1 = [op("s", [k_far1[b]], lambda: S.activation(xs(far[0], b, 2), bank(4 + b, 128), F.Copy)) for b in (1, 3)]
+    k_fv2 = [op("s", [k_far2[b]], lambda: S.activation(xs(far[2], b, 2), bank(b, 128), F.Copy)) for b in range(4)]
 
-    k_sum = []
     k = k_x0
     for s in range(N):
         if s == far[0]:
-            k_fv += [op("v", [k_far[b]], lambda: V.tensor_copy(xs(far[0], b, 4), bank(4 + b, 256))) for b in (0, 1)]
+            k_offf = final_offsets()
+            k_fv1 += [op("v", [k_far1[b]], lambda: V.tensor_copy(xs(far[0], b, 2), bank(4 + b, 128))) for b in (0, 2)]
             for r in far:
-                k_ready[r] = k_fv
+                k_ready[r] = k_fv1 if r in far[:2] else k_fv2
         if s:
             a = 8 + 256 * s
             k = op("v", [k, k_offc, k_x0] + k_ready[s] + k_ready[0] + k_d, lambda: V.tensor_tensor(
                 T.x[:, a:a + 256], T.x[:, 0:a].indirect(T.offc[:, 16 * (s - 1):16 * s]), T.x[:, a:a + 256], A.add))
-    for i in range(4):
-        e = "v" if i % 2 == 0 else "s"
-        out, src = T.ac[:, 512 * i:512 * i + 512], T.x[:, 0:2056].indirect(T.offf[:, 32 * i:32 * i + 32])
+    for e, y, a, b in (("v", "y", 0, 384), ("s", "y", 384, 768), ("v", "y", 768, 1408), ("s", "s", 1408, 2048)):
+        out, src = T.ac[:, a:b], T.x[:, 0:2056].indirect(T.offf[:, a // 16:b // 16])
         if e == "v":
             ka = op("v", [k, k_offf], lambda: V.tensor_copy(out, src))
         else:
             ka = op("s", [k, k_offf], lambda: S.activation(out, src, F.Copy))
-        store("y" if i != 3 else "s", [ka], T.acc[:, 512 * i:512 * i + 512], out)
+        store(y, [ka], T.acc[:, a:b], out)
 
-    need("p", [("q" + e, count[e]) for e in "vstp"] + [("st", count["st"]), ("loc", 3 * (len(far_e) + len(near_e)))])
+    need("p", [("q" + e, count[e]) for e in "vstp"] + [("st", count["st"]), left])

from concourse.bass import DstId, RemoteDMATransfer
from concourse.mybir import dt, AluOpType, AxisListType, ActivationFunctionType

A = AluOpType
F = ActivationFunctionType
AX = AxisListType.X
STEP = 4096.0
DROP = 1048576.0

SCRATCH = {
    "grt": ("sbuf", [128, 2048], "bfloat16"),
    "uc": ("sbuf", [128, 16], "bfloat16"),
    "ut": ("sbuf", [128, 512], "bfloat16"),
    "uq": ("sbuf", [128, 128], "float8_e4m3fn_x4"),
    "us": ("sbuf", [128, 128], "uint8"),
    "gq": ("sbuf", [128, 512], "float8_e4m3fn_x4"),
    "gs": ("sbuf", [128, 512], "uint8"),
    "ones": ("sbuf", [128, 128], "bfloat16"),
    "ident": ("sbuf", [128, 128], "bfloat16"),
    "et": ("sbuf", [128, 2048], "bfloat16"),
    "eq": ("sbuf", [128, 512], "float8_e4m3fn_x4"),
    "es": ("sbuf", [128, 512], "uint8"),
    "pi": ("sbuf", [128, 32], "int32"),
    "p3": ("sbuf", [128, 32], "int32"),
    "ic": ("sbuf", [128, 4], "int32"),
    "fc": ("sbuf", [128, 4], "float32"),
    "uoff": ("sbuf", [128, 32], "uint16"),
    "j0": ("sbuf", [128, 64], "float32"),
    "jt": ("sbuf", [128, 64], "float32"),
    "m0": ("sbuf", [128, 64], "float32"),
    "md": ("sbuf", [128, 64], "float32"),
    "n0": ("sbuf", [128, 512], "float32"),
    "n1": ("sbuf", [128, 512], "float32"),
    "stp": ("sbuf", [128, 512], "float32"),
    "cor": ("sbuf", [128, 1], "float32"),
    "sl0": ("sbuf", [128, 512], "float32"),
    "slot": ("sbuf", [128, 512], "float32"),
    "pt": ("sbuf", [128, 512], "float32"),
    "pv": ("sbuf", [128, 512], "float32"),
    "pts": ("sbuf", [128, 512], "float32"),
    "pvs": ("sbuf", [128, 448], "float32"),
    "sabs": ("sbuf", [128, 512], "float32"),
    "scol": ("sbuf", [128, 4], "float32"),
    "eqt": ("sbuf", [128, 512], "float32"),
    "eqm": ("sbuf", [128, 512], "float32"),
    "cmp": ("sbuf", [128, 2048], "float32"),
    "cnt": ("sbuf", [128, 8], "float32"),
    "eqc": ("sbuf", [128, 4], "float32"),
    "ru": ("sbuf", [128, 4], "uint16"),
    "w": ("sbuf", [128, 512], "float32"),
    "t1": ("sbuf", [128, 64], "float32"),
    "xp": ("sbuf", [128, 64], "float32"),
    "yr": ("sbuf", [128, 64], "float32"),
    "bb": ("sbuf", [128, 256], "float32"),
    "bm": ("sbuf", [128, 256], "float32"),
    "lf": ("sbuf", [128, 32], "float32"),
    "lx": ("sbuf", [128, 32], "uint16"),
    "lown": ("sbuf", [128, 4], "uint16"),
    "ou": ("sbuf", [128, 16], "uint16"),
    "h": ("sbuf", [128, 512], "bfloat16"),
    "hq": ("sbuf", [128, 128], "float8_e4m3fn_x4"),
    "hs": ("sbuf", [128, 128], "uint8"),
    "ql": ("sbuf", [128, 192], "float8_e4m3fn_x4"),
    "pl": ("sbuf", [128, 192], "uint8"),
    "qr": ("sbuf", [128, 256], "float8_e4m3fn_x4"),
    "pr": ("sbuf", [128, 256], "uint8"),
    "e32": ("sbuf", [128, 2048], "float32"),
    "d": ("sbuf", [128, 256], "float32"),
    "scg": ("sbuf", [128, 64], "float32"),
    "scp": ("sbuf", [128, 64], "float32"),
    "x": ("sbuf", [128, 2056], "float32"),
    "offc": ("sbuf", [128, 112], "uint16"),
    "offf": ("sbuf", [128, 128], "uint16"),
    "ac": ("sbuf", [128, 2048], "float32"),
    "ps": ("psum", [128, 4096], "float32"),
}
SEMAPHORES = ["qv", "qs", "qt", "qp", "lu", "l0", "l1", "st", "ll", "lr", "cl", "cr", "loc"]


def rank_program(g, core, T, topo):
    rank = T.rank_of(core)
    if rank is None:
        return
    N = len(T.cores)
    near = [r for r in range(N) if topo.chip(T.cores[r]) == topo.chip(core)]
    far = [r for r in range(N) if r not in near]
    near_others = [r for r in near if r != rank]

    queue = {"v": g.vector, "s": g.scalar, "t": g.tensor, "p": g, "y": g.sync}
    count = {"v": 0, "s": 0, "t": 0, "p": 0, "st": 0}
    seen = {}

    def need(e, deps):
        top = {}
        for sem, val in deps:
            top[sem] = max(val, top.get(sem, 0))
        for sem in top:
            if seen.get((e, sem), 0) < top[sem]:
                queue[e].wait_ge(T.sem[sem], top[sem])
                seen[(e, sem)] = top[sem]

    def op(e, deps, call):
        need(e, deps)
        count[e] += 1
        call().then_inc(T.sem["q" + e], 1)
        return ("q" + e, count[e])

    def load(e, out, in_, sem):
        queue[e].dma_start(out, in_).then_inc(T.sem[sem], 16)
        return (sem, 16)

    def store(e, deps, out, in_):
        need(e, deps)
        queue[e].dma_start(out, in_).then_inc(T.sem["st"], 16)
        count["st"] += 16

    V, S = g.vector, g.scalar

    def bank(b, n):
        return T.ps[:, 512 * b:512 * b + n]

    def vs(deps, out, in0, s1, op0, s2=None, op1=None):
        if op1 is None:
            return op("v", deps, lambda: V.tensor_scalar(out=out, in0=in0, scalar1=s1, scalar2=None, op0=op0))
        return op("v", deps, lambda: V.tensor_scalar(out=out, in0=in0, scalar1=s1, scalar2=s2, op0=op0, op1=op1))

    lu = load("y", T.uc[:, 0:16], T.u[:, 0:16], "lu")
    l0 = load("y", T.grt[:, 0:1024], T.gr[:, 0:1024], "l0")
    l1 = load("y", T.grt[:, 1024:2048], T.gr[:, 1024:2048], "l1")

    def whole(out, pattern, base=0):
        return op("p", [], lambda: g.iota(out, pattern, base, 0, allow_small_or_imprecise_dtypes=True))
    k_pi = op("p", [], lambda: g.iota(T.pi[:, 0:32], [[0, 32]], 0, 1))
    k_ones = op("v", [], lambda: V.memset(T.ones[:, :], 1.0))
    k_id = op("p", [k_ones], lambda: g.affine_select(T.ident[:, :], T.ones[:, :], [[-1, 128]], A.is_equal, 0.0, 0, 1))
    k_j0 = whole(T.j0[:, :], [[128, 4], [1, 16]])
    k_m0 = whole(T.m0[:, :], [[1, 16], [0, 4]])
    k_sl0 = whole(T.sl0[:, :], [[4, 512]], 8)
    k_n0 = whole(T.n0[:, :], [[0, 128], [4, 4]])

    k_p3 = vs([k_pi], T.p3[:, :], T.pi[:, :], 3, A.bitwise_and)
    for i, bits in ((0, 3), (1, 12), (2, 112), (3, 15)):
        k_ic = vs([k_pi], T.ic[:, i:i + 1], T.pi[:, 0:1], bits, A.bitwise_and)
    k_uoff = op("v", [k_p3], lambda: V.tensor_copy(T.uoff[:, :], T.p3[:, :]))
    k_fc = op("v", [k_ic], lambda: V.tensor_copy(T.fc[:, :], T.ic[:, :]))
    k_et = op("v", [], lambda: V.memset(T.et[:, :], 0.0))
    k_e = [op("s", [k_id, k_et], lambda: S.activation(T.et[:, 512 * b + b:512 * (b + 1):4], T.ident[:, :], F.Copy)) for b in range(4)]
    k_slot = op("s", [k_sl0, k_fc], lambda: S.activation(T.slot[:, :], T.sl0[:, :], F.Identity, bias=T.fc[:, 0:1]))
    k_pt = op("s", [k_sl0, k_fc], lambda: S.activation(T.pt[:, :], T.sl0[:, :], F.Identity, bias=T.fc[:, 0:1], scale=0.0))

    k_ut = op("v", [lu, k_uoff], lambda: V.tensor_copy(T.ut[:, :], T.uc[:, 0:16].indirect(T.uoff[:, 0:32])))
    k_uq = op("v", [k_ut], lambda: V.quantize_mx(T.uq[:, 0:128], T.us[:, 0:128], T.ut[:, 0:512]))

    def pack(a, ld):
        return op("v", [ld], lambda: V.quantize_mx(T.gq[:, a:a + 256], T.gs[:, a:a + 256], T.grt[:, 4 * a:4 * a + 1024]))
    k_g = [pack(0, l0)]
    k_w = op("v", [], lambda: V.memset(T.w[:, 0:64], 0.0))
    k_xp = op("v", [], lambda: V.memset(T.xp[:, :], 0.0))
    k_jt = vs([k_j0, k_fc], T.jt[:, :], T.j0[:, :], T.fc[:, 2:3], A.add)
    k_md = vs([k_m0, k_fc], T.md[:, :], T.m0[:, :], T.fc[:, 3:4], A.is_equal)
    k_g.append(pack(256, l1))
    k_c0 = op("s", [l0], lambda: S.activation(T.e32[:, 0:512], T.grt[:, 0:512], F.Copy))
    k_abs, k_sc = [], []
    for i, b in ((0, 0), (1, 5)):
        a = 256 * i
        k = op("t", [k_uq, k_g[i]], lambda: g.tensor.matmul_mx(bank(b, 256), T.uq[:, 0:128], T.us[:, 0:128], T.gq[:, a:a + 256], T.gs[:, a:a + 256], True, True))
        k_abs.append(op("s", [k], lambda: S.activation(T.sabs[:, a:a + 256], bank(b, 256), F.Abs)))
        for q in (2 * i, 2 * i + 1):
            k_sc.append(op("t", [k_uq, k_g[i]], lambda: g.tensor.matmul_mx(
                bank(1 + q, 128), T.gq[:, 128 * q:128 * q + 128], T.gs[:, 128 * q:128 * q + 128], T.uq[:, 0:128], T.us[:, 0:128], True, True)))

    k_scol, k_eq, k_cnt = [], [], {}

    def column_score(q):
        k_scol.append(op("v", [k_sc[q]], lambda: V.tensor_reduce(T.scol[:, q:q + 1], bank(1 + q, 1), AX, A.max, apply_absolute_value=True)))

    def equal_scores(q):
        k_eq.append(vs([k_abs[q // 2], k_scol[q]], T.eqt[:, 128 * q:128 * q + 128], T.sabs[:, 128 * q:128 * q + 128], T.scol[:, q:q + 1], A.is_equal))

    def larger_scores(q, i):
        lo, hi = 256 * i, 256 * i + 256
        cut = min(max(128 * q, lo), hi)
        for a, b, how in ((lo, cut, A.is_ge), (cut, hi, A.is_gt)):
            if a < b:
                k = vs([k_abs[i], k_scol[q]], T.cmp[:, 512 * q + a:512 * q + b], T.sabs[:, a:b], T.scol[:, q:q + 1], how)
        part = T.cmp[:, 512 * q + lo:512 * q + hi]
        k_cnt[(q, i)] = op("s", [k], lambda: S.activation(part, part, F.Copy, accum_out=T.cnt[:, 4 * i + q:4 * i + q + 1]))
    for q in (0, 1):
        column_score(q)
    for q in (0, 1):
        equal_scores(q)
    for q in (0, 1):
        larger_scores(q, 0)
    for q in (2, 3):
        column_score(q)
    for q in (2, 3):
        equal_scores(q)
    k_eqm = op("p", k_eq, lambda: g.affine_select(T.eqm[:, :], T.eqt[:, :], [[0, 4], [-1, 128]], A.is_gt, 0.0, 0, 1))
    for q, i in ((0, 1), (1, 1), (2, 0), (2, 1), (3, 0), (3, 1)):
        larger_scores(q, i)

    def eq_part(q):
        return T.eqm[:, 128 * q:128 * q + 128]
    k_eqc = [op("v", [k_eqm], lambda: V.tensor_reduce(T.eqc[:, q:q + 1], eq_part(q), AX, A.add)) for q in range(3)]
    k_eqc.append(op("s", [k_eqm], lambda: S.activation(eq_part(3), eq_part(3), F.Copy, accum_out=T.eqc[:, 3:4])))
    k_ru = [vs([k_cnt[(q, 0)], k_cnt[(q, 1)], k_eqc[q]], T.ru[:, q:q + 1], T.cnt[:, q:q + 1], T.cnt[:, 4 + q:5 + q], A.add, T.eqc[:, q:q + 1], A.add) for q in range(4)]

    k_c1 = op("s", [l0, l1], lambda: S.activation(T.e32[:, 512:2048], T.grt[:, 512:2048], F.Copy))

    k_w1 = op("v", [k_w, k_jt] + k_ru, lambda: V.tensor_copy(T.w[:, 0:512].indirect(T.ru[:, 0:4]), T.jt[:, 0:64]))
    k_t1 = op("v", [k_w1], lambda: V.transpose(T.t1[:, :], T.w[:, 0:64]))
    k_x1 = op("v", [k_t1, k_xp], lambda: V.tensor_tensor(T.xp[:, 0:64:32], T.t1[:, 0:64:32], T.t1[:, 16:64:32], A.add))
    k_y = op("v", [k_x1], lambda: V.transpose(T.yr[:, :], T.xp[:, :]))
    k_h0 = op("v", [], lambda: V.memset(T.h[:, 256:512], 0.0))
    k_x0 = op("v", [], lambda: V.memset(T.x[:, 0:8], 0.0))
    k_cor = vs([k_fc], T.cor[:, :], T.fc[:, 1:2], STEP / 4, A.mult, -3 * STEP, A.add)
    k_bm = []
    for a in range(4):
        k = op("p", [k_y], lambda: g.partition_broadcast(T.bb[:, 64 * a:64 * a + 64], T.yr[32 * a:32 * a + 1, 0:64], 128))
        k_bm.append(op("v", [k, k_md], lambda: V.tensor_tensor(T.bm[:, 64 * a:64 * a + 64], T.bb[:, 64 * a:64 * a + 64], T.md[:, :], A.mult)))
        if a == 0:
            k_eqz = op("v", k_e, lambda: V.quantize_mx(T.eq[:, 0:512], T.es[:, 0:512], T.et[:, 0:2048]))
    own = 4 * rank
    k_lf = [op("v", k_bm, lambda: V.tensor_reduce(T.lf[:, own + c:own + c + 1], T.bm[:, c:256:4], AX, A.add)) for c in range(4)]

    far_e = topo.engines(core, T.cores[far[0]])
    near_e = [e for e in topo.engines(core, T.cores[near_others[0]]) if e not in far_e]
    far_mask = sum(1 << e for e in far_e)
    near_mask = sum(1 << e for e in near_e)
    left = ("loc", 3 * (len(far_e) + len(near_e)))

    def ids(ranks):
        return [DstId(rid=topo.addr(T.cores[r])[0], pnc=topo.addr(T.cores[r])[1]) for r in ranks]

    def near_at(r):
        return [q for q in near if q != r].index(rank)

    def send(deps, src, near_dst, far_dst, near_sem, far_sem):
        need("p", deps)
        g.remote_dma_fused([
            RemoteDMATransfer(dst_ids=ids(far), dma_engine_mask=far_mask, remote_sem=T.sem[far_sem], srcs=[src], dsts=[far_dst(r) for r in far]),
            RemoteDMATransfer(dst_ids=ids(near_others), dma_engine_mask=near_mask, remote_sem=T.sem[near_sem], srcs=[src], dsts=[near_dst(r) for r in near_others]),
        ], local_sem=T.sem["loc"])

    send(k_lf, T.lf[:, own:own + 4], lambda r: T.lf[:, own:own + 4], lambda r: T.lf[:, own:own + 4], "ll", "lr")
    ll = ("ll", len(near_others) * len(near_e))
    lr = ("lr", len(far) * len(far_e))

    k_ou = {t: vs(k_lf, T.ou[:, 4 * t:4 * t + 4], T.lf[:, own:own + 4], 4.0, A.mult, float(t), A.add) for t in (2, 0, 3, 1)}
    k_h = []
    for t in (2, 3):
        k_h.append(op("s", [k_ou[t], l0, l1], lambda: S.activation(T.h[:, t:256:4], T.grt[:, 0:2048].indirect(T.ou[:, 4 * t:4 * t + 4]), F.Copy)))
    for t in (0, 1):
        k_h.append(op("v", [k_ou[t], l0, l1], lambda: V.tensor_copy(T.h[:, t:256:4], T.grt[:, 0:2048].indirect(T.ou[:, 4 * t:4 * t + 4]))))
    k_hq = op("v", k_h + [k_h0], lambda: V.quantize_mx(T.hq[:, 0:128], T.hs[:, 0:128], T.h[:, 0:512]))

    fa = 64 * near.index(rank)
    send([k_hq], T.hq[:, 0:64].bitcast(dt.uint8),
         lambda r: T.ql[:, 64 * near_at(r):64 * near_at(r) + 64].bitcast(dt.uint8),
         lambda r: T.qr[:, fa:fa + 64].bitcast(dt.uint8), "cl", "cr")
    send([k_hq], T.hs[:, 0:64],
         lambda r: T.pl[:, 64 * near_at(r):64 * near_at(r) + 64],
         lambda r: T.pr[:, fa:fa + 64], "cl", "cr")
    cl = ("cl", 2 * len(near_others) * len(near_e))
    cr = ("cr", 2 * len(far) * len(far_e))

    def unpack(b, to, q, s, a, n, deps):
        return op("t", deps + [k_eqz], lambda: g.tensor.matmul_mx(bank(to, n), T.eq[:, 128 * b:128 * b + 128], T.es[:, 128 * b:128 * b + 128], q[:, a:a + n], s[:, a:a + n], True, True))

    def xs(r, b, n):
        return T.x[:, 8 + 256 * r + b:8 + 256 * (r + n):4]
    k_own = [unpack(b, 4 + b, T.hq, T.hs, 0, 128, [k_hq] + k_scol + k_abs) for b in range(4)]
    k_xo = [op("s", [k_own[b]], lambda: S.activation(xs(rank, b, 1), bank(4 + b, 64), F.Copy)) for b in range(4)]
    k_lown = op("v", k_lf, lambda: V.tensor_copy(T.lown[:, :], T.lf[:, own:own + 4]))
    k_n1 = vs([k_n0, k_fc], T.n1[:, :], T.n0[:, :], T.fc[:, 1:2], A.is_equal, -(DROP + STEP), A.mult)
    k_d = [op("v", [k_xo[b]] + k_h, lambda: V.tensor_tensor(T.d[:, 64 * b:64 * b + 64], T.h[:, b:256:4], xs(rank, b, 1), A.subtract)) for b in range(4)]
    k_er = op("v", k_d + [k_c0, k_c1] + [k_ou[t] for t in range(4)], lambda: V.tensor_copy(T.e32[:, 0:2048].indirect(T.ou[:, 0:16]), T.d[:, 0:256]))

    k_scg = op("s", [k_lown] + k_abs, lambda: S.activation(T.scg[:, :], T.sabs[:, 0:512].indirect(T.lown[:, 0:4]), F.Copy))
    k_scp = [op("s", [k_scg], lambda: S.activation(T.scp[0:1, c:64:4], T.scg[0:1, 16 * c:16 * c + 16], F.Copy)) for c in range(4)]
    store("y", k_scp, T.sc[:, :], T.scp[0:1, 0:64])
    k_stp = op("s", [k_n1], lambda: S.activation(T.stp[:, :], T.n1[:, :], F.Identity, bias=STEP))

    k_lx = {}
    for part, arrived in ((near, ll), (far, lr)):
        a = 4 * part[0]
        k = op("v", [arrived] + (k_lf if part is near else []), lambda: V.tensor_copy(T.lx[:, a:a + 16], T.lf[:, a:a + 16]))
        for r in part:
            k_lx[r] = k
    k_tab = k_pt
    for s in range(N):
        lst = T.lx[:, 4 * s:4 * s + 4]
        if s:
            k_tab = op("v", [k_tab, k_lx[s]], lambda: V.tensor_copy(T.pv[:, 64 * s:64 * s + 64], T.pt[:, 0:512].indirect(lst)))
            k_pv = k_tab
        k_tab = op("v", [k_tab, k_lx[s], k_slot], lambda: V.tensor_copy(T.pt[:, 0:512].indirect(lst), T.slot[:, 64 * s:64 * s + 64]))
    k_pvs = op("v", [k_pv, k_stp], lambda: V.tensor_tensor_scan(T.pvs[:, 0:448], T.stp[:, 0:448], T.pv[:, 64:512], 0.0, A.add, A.max))
    k_offc = vs([k_pvs, k_cor], T.offc[:, 0:112], T.pvs[:, 3:448:4], T.cor[:, 0:1], A.add)

    def final_offsets():
        k = op("v", [k_tab, k_stp], lambda: V.tensor_tensor_scan(T.pts[:, 0:512], T.stp[:, 0:512], T.pt[:, 0:512], 0.0, A.add, A.max))
        return vs([k, k_cor], T.offf[:, 0:128], T.pts[:, 3:512:4], T.cor[:, 0:1], A.add)
    for s in near + far:
        store("y", k_lf if s == rank else [ll if s in near else lr], T.nb[s:s + 1, 0:64], T.lf[0:16, 4 * s:4 * s + 4])
    store("y", [k_er, left], T.er[:, 0:1024], T.e32[:, 0:1024])
    store("y", [k_er, left], T.er[:, 1024:2048], T.e32[:, 1024:2048])

    k_near = [unpack(b, b, T.ql, T.pl, 0, 192, [cl] + k_abs + k_scol) for b in range(4)]
    k_v = []
    for b in range(4):
        i = near.index(rank)
        for at, first, n in ((0, near[0], i), (i, rank + 1, len(near) - 1 - i)):
            if n:
                k_v.append(op("s", [k_near[b]], lambda: S.activation(xs(first, b, n), T.ps[:, 512 * b + 64 * at:512 * b + 64 * (at + n)], F.Copy)))
    k_far1 = [unpack(b, 4 + b, T.qr, T.pr, 0, 128, [cr] + k_xo) for b in range(4)]
    k_far2 = [unpack(b, b, T.qr, T.pr, 128, 128, [cr] + k_v) for b in range(4)]
    k_v += k_xo
    k_ready = {r: k_v for r in near}
    k_fv1 = [op("s", [k_far1[b]], lambda: S.activation(xs(far[0], b, 2), bank(4 + b, 128), F.Copy)) for b in (1, 3)]
    k_fv2 = [op("s", [k_far2[b]], lambda: S.activation(xs(far[2], b, 2), bank(b, 128), F.Copy)) for b in range(4)]

    k = k_x0
    for s in range(N):
        if s == far[0]:
            k_offf = final_offsets()
            k_fv1 += [op("v", [k_far1[b]], lambda: V.tensor_copy(xs(far[0], b, 2), bank(4 + b, 128))) for b in (0, 2)]
            for r in far:
                k_ready[r] = k_fv1 if r in far[:2] else k_fv2
        if s:
            a = 8 + 256 * s
            k = op("v", [k, k_offc, k_x0] + k_ready[s] + k_ready[0] + k_d, lambda: V.tensor_tensor(
                T.x[:, a:a + 256], T.x[:, 0:a].indirect(T.offc[:, 16 * (s - 1):16 * s]), T.x[:, a:a + 256], A.add))
    for e, y, a, b in (("v", "y", 0, 384), ("s", "y", 384, 768), ("v", "y", 768, 1408), ("s", "s", 1408, 2048)):
        out, src = T.ac[:, a:b], T.x[:, 0:2056].indirect(T.offf[:, a // 16:b // 16])
        if e == "v":
            ka = op("v", [k, k_offf], lambda: V.tensor_copy(out, src))
        else:
            ka = op("s", [k, k_offf], lambda: S.activation(out, src, F.Copy))
        store(y, [ka], T.acc[:, a:b], out)

    need("p", [("q" + e, count[e]) for e in "vstp"] + [("st", count["st"]), left])
